import numpy as np
import ml_dtypes


def mxq(x, axis, fmt="e4m3"):
    dtype, down = {"e4m3": (ml_dtypes.float8_e4m3fn, 7), "e5m2": (ml_dtypes.float8_e5m2, 14)}[fmt]
    v = np.moveaxis(np.asarray(x, np.float32).astype(ml_dtypes.bfloat16).astype(np.float64), axis, -1)
    blocks = v.reshape(v.shape[:-1] + (-1, 32))
    amax = np.abs(blocks).max(-1, keepdims=True)
    byte = np.maximum(np.where(amax > 0, np.frexp(amax)[1] - 1 + 127, 0) - down, 1)
    scale = np.exp2(byte - 127.0)
    codes = (blocks / scale).astype(np.float32).astype(dtype).astype(np.float64)
    return np.moveaxis((codes * scale).reshape(v.shape), -1, axis)


WIDE = False


def mx_kscale(k):
    if not WIDE:
        return np.ones(k)
    levels = np.array([10, -10, 5, -5, 0])
    if k % 512:
        return np.exp2(np.random.permutation(np.resize(levels, k // 32))).repeat(32)
    a = np.empty((k // 512, 16))
    for p in range(k // 512):
        a[p, :8] = np.random.permutation(np.resize(levels, 8))
        for g in range(8):
            far = levels[np.abs(levels - a[p, g]) >= 10]
            a[p, g + 8] = far[np.random.randint(len(far))]
    return np.exp2(a.ravel()).repeat(32)


def f64(x):
    return np.asarray(x).astype(np.float64)


def striped(idx):
    return np.tile(idx.reshape(-1, 16).T, (8, 1)).astype(np.uint16)


def unstriped(offs):
    return offs[:16].T.reshape(-1).astype(np.int64)


def pack_weight(w):
    k, n = w.shape
    w = f64(np.asarray(w, np.float32).astype(ml_dtypes.bfloat16)).reshape(k // 32, 32, n)
    amax = np.abs(w).max(1)
    byte = np.clip(np.where(amax > 0, np.frexp(amax)[1] - 1 + 127 - 7, 1), 1, 254)
    scaled = (w * np.exp2(127.0 - byte)[:, None, :]).reshape(k, n).astype(np.float32)
    words = np.ascontiguousarray(scaled.reshape(k // 512, 128, 4, n).transpose(0, 1, 3, 2)).astype(ml_dtypes.float8_e4m3fn).view(np.uint8)
    return words, np.ascontiguousarray(byte.astype(np.uint8).reshape(k // 512, 16, n))


def unpack_weight(words, scales):
    g, p, n, _ = words.shape
    vals = np.ascontiguousarray(words).view(ml_dtypes.float8_e4m3fn).astype(np.float64) * np.repeat(np.exp2(scales.astype(np.float64) - 127.0), 8, axis=1)[..., None]
    return vals.transpose(0, 1, 3, 2).reshape(g * 512, n)


K, T, E, C, N = 1024, 512, 2, 256, 512


def by_expert(wq, xq):
    return np.concatenate([wq[e].T @ xq[:, e * C:(e + 1) * C] for e in range(E)], axis=1)


def setup_inputs():
    n = np.random.standard_normal
    s = mx_kscale(K)[:, None]
    packed = [pack_weight(m) for m in n((E, K, N)) / np.sqrt(K) / s[None]]
    return {
        "xT": (n((K, T)) * s).astype(np.float32),
        "w_words": np.stack([m[0] for m in packed]),
        "w_scales": np.stack([m[1] for m in packed]),
        "gate": np.tile(np.random.uniform(0.2, 1.0, E * C), (N, 1)).astype(np.float32),
        "offs": striped(np.random.permutation(T)[:E * C]),
    }


def reference(xT, w_words, w_scales, gate, offs):
    idx = unstriped(offs)
    xq = mxq(f64(xT)[:, idx], 0, "e4m3")
    w = np.stack([unpack_weight(w_words[e], w_scales[e]) for e in range(E)])
    y = by_expert(w, xq)
    out = np.zeros((N, T))
    out[:, idx] = f64(gate) * y
    return out

@@ -1,0 +1,194 @@
+from contextlib import ExitStack
+
+import concourse.mybir as mybir
+
+K, T, E, C, N = 1024, 512, 2, 256, 512
+FLOPS = 2 * K * N * E * C
+
+F32 = mybir.dt.float32
+BF16 = mybir.dt.bfloat16
+U32 = mybir.dt.uint32
+I32 = mybir.dt.int32
+U16 = mybir.dt.uint16
+U8 = mybir.dt.uint8
+FP8X4 = mybir.dt.float8_e4m3fn_x4
+MULT = mybir.AluOpType.mult
+ADD = mybir.AluOpType.add
+COPY = mybir.ActivationFunctionType.Copy
+
+P = 128
+PASSES = K // 512
+BLOCKS = N // P
+LIST_COLS = C // 16
+
+
+def tile_routed_moe_kernel(tc, xT, w_words, w_scales, gate, offs, out):
+    nc = tc.nc
+    with ExitStack() as ctx:
+        lists = ctx.enter_context(tc.tile_pool(name="lists", bufs=1))
+        keep = ctx.enter_context(tc.tile_pool(name="keep", bufs=1))
+        psum = ctx.enter_context(tc.psum_pool(name="psum", bufs=1))
+
+        offsets = lists.tile([P, E * C // 16], U16, name="offsets")
+
+        def slots(e):
+            return offsets[:, e * LIST_COLS : (e + 1) * LIST_COLS]
+
+        warm = keep.tile([P, 2], F32, name="warm")
+        nc.vector.memset(warm[:, 0:1], 0.0)
+        nc.scalar.copy(warm[:, 1:2], warm[:, 0:1])
+
+        w_planes = keep.tile([P, N], U8, name="w_planes", align_bytes=64)
+        nc.vector.memset(w_planes[:].bitcast(I32), 0)
+
+        x_rows = xT.rearrange("(g p t) n -> g p t n", p=P, t=4)
+        raw = {}
+        for u in range(2):
+            for g in range(PASSES):
+                raw[g, u] = keep.tile([P, 2, T], F32, name="raw%d%d" % (g, u))
+                nc.sync.dma_start(raw[g, u][:], x_rows[g, :, 2 * u : 2 * u + 2, :])
+                if (g, u) == (0, 0):
+                    nc.sync.dma_start(offsets[:], offs)
+
+        s_rows = w_scales.rearrange("e a q n -> (e a) q n")
+        for q in range(4):
+            nc.sync.dma_start(
+                w_planes[32 * q : 32 * q + 16, :].bitcast(I32),
+                s_rows[:, 4 * q : 4 * q + 4, :].bitcast(I32),
+            )
+        w_codes = keep.tile([P, E * PASSES, N], U32, name="w_codes", align_bytes=64)
+        gates = keep.tile([P, BLOCKS, E * C], F32, name="gates")
+        nc.sync.dma_start(
+            w_codes[:, 0:PASSES, :].bitcast(I32),
+            w_words[0].rearrange("a p n r -> p a (n r)").bitcast(I32),
+        )
+        nc.sync.dma_start(gates[:], gate.rearrange("(b p) j -> p b j", p=P))
+        nc.sync.dma_start(
+            w_codes[:, PASSES : 2 * PASSES, :].bitcast(I32),
+            w_words[1].rearrange("a p n r -> p a (n r)").bitcast(I32),
+        )
+
+        grouped = {}
+        x_codes = {}
+        x_planes = {}
+
+        def new_grouped(g, e, tag):
+            grouped[g, e] = keep.tile([P, C, 4], BF16, name="grouped%d%d" % (g, e), tag=tag, align_bytes=64)
+
+        planes = {}
+
+        def plane_cast(u):
+            planes[u] = keep.tile([P, 2, T], BF16, name="planes%d" % u, tag="planes%d" % u, align_bytes=64)
+            if u == 0:
+                nc.vector.tensor_copy(out=planes[u][:], in_=raw[0, u][:])
+            else:
+                nc.gpsimd.tensor_scalar(planes[u][:], raw[0, u][:], 1.0, 0.0, MULT, ADD)
+
+        def scalar_gather(e, u):
+            for h in range(2):
+                nc.scalar.activation(grouped[0, e][:, :, 2 * u + h], planes[u][:, h, :].indirect(slots(e)), COPY)
+
+        pair = {}
+
+        def pair_cast(u):
+            pair[u] = keep.tile([P, T, 2], BF16, name="pair%d" % u, align_bytes=64)
+            nc.vector.tensor_copy(out=pair[u][:], in_=raw[1, u][:].rearrange("p h n -> p n h"))
+
+        def vector_gather(e, u):
+            words = grouped[1, e][:].rearrange("p c t -> p (c t)").bitcast(U32)
+            nc.vector.tensor_copy(
+                words.rearrange("p (c u) -> p c u", u=2)[:, :, u],
+                pair[u][:].rearrange("p n h -> p (n h)").bitcast(U32).indirect(slots(e)),
+            )
+
+        def late_planes():
+            planes[2] = keep.tile([P, 2, T], BF16, name="planes2", align_bytes=64)
+            nc.gpsimd.tensor_scalar(planes[2][:], raw[1, 1][:], 1.0, 0.0, MULT, ADD)
+
+        def late_gather():
+            for h in range(2):
+                nc.scalar.activation(grouped[1, 1][:, :, 2 + h], planes[2][:, h, :].indirect(slots(1)), COPY)
+
+        def quantize(g, e, tag):
+            x_codes[g, e] = keep.tile([P, C], U32, name="x_codes%d%d" % (g, e), tag=tag, align_bytes=64)
+            x_planes[g, e] = keep.tile([P, C], U8, name="x_planes%d%d" % (g, e), align_bytes=64)
+            nc.vector.quantize_mx(
+                out=x_codes[g, e][:].bitcast(FP8X4),
+                scales=x_planes[g, e][:],
+                in_=grouped[g, e][:].rearrange("p c t -> p (c t)"),
+            )
+
+        acc = {}
+        for e in range(E):
+            for b in range(BLOCKS):
+                acc[e, b] = psum.tile([P, C], F32, name="acc%d%d" % (e, b))
+
+        def multiply_block(e, g, b, opens):
+            j = e * PASSES + g
+            cols = slice(b * P, (b + 1) * P)
+            nc.tensor.matmul_mx(
+                out=acc[e, b][:],
+                lhsT=w_codes[:, j, cols].bitcast(FP8X4),
+                lhsT_scale=w_planes[4 * j : P, cols],
+                rhs=x_codes[g, e][:].bitcast(FP8X4),
+                rhs_scale=x_planes[g, e][:],
+                start=opens,
+                stop=not opens,
+            )
+
+        def multiply(e, g, opens):
+            for b in range(BLOCKS):
+                multiply_block(e, g, b, opens)
+
+        windows = {}
+        for b in range(BLOCKS):
+            windows[b] = keep.tile([P, T], F32, name="window%d" % b)
+        sums = {}
+
+        def empty(e, b):
+            sums[e, b] = keep.tile([P, C], F32, name="sums%d%d" % (e, b), tag=("planes1" if (e, b) == (0, 3) else "sums%d%d" % (e, b)), align_bytes=64)
+            nc.scalar.copy(sums[e, b][:], acc[e, b][:])
+
+        def scatter(e, b):
+            nc.vector.tensor_tensor(windows[b][:].indirect(slots(e)), sums[e, b][:], gates[:, b, e * C : (e + 1) * C], MULT)
+            if e == E - 1:
+                nc.sync.dma_start(out[b * P : (b + 1) * P, :], windows[b][:])
+
+        new_grouped(0, 0, "slot_b")
+        new_grouped(1, 0, "slot_a")
+        plane_cast(0)
+        scalar_gather(0, 0)
+        pair_cast(0)
+        vector_gather(0, 0)
+        new_grouped(1, 1, "slot_d")
+        vector_gather(1, 0)
+        plane_cast(1)
+        scalar_gather(0, 1)
+        pair_cast(1)
+        late_planes()
+        vector_gather(0, 1)
+        quantize(1, 0, "slot_c")
+        multiply_block(0, 1, 0, True)
+        quantize(0, 0, "slot_a")
+        multiply_block(0, 0, 0, False)
+        for b in range(1, BLOCKS):
+            multiply_block(0, 0, b, True)
+            multiply_block(0, 1, b, False)
+        late_gather()
+        quantize(1, 1, "codes11")
+        multiply(1, 1, True)
+        for b in range(BLOCKS - 1):
+            empty(0, b)
+        new_grouped(0, 1, "slot_c")
+        scalar_gather(1, 0)
+        scalar_gather(1, 1)
+        empty(0, 3)
+        scatter(0, 0)
+        scatter(0, 1)
+        scatter(0, 2)
+        quantize(0, 1, "codes01")
+        multiply(1, 0, False)
+        scatter(0, 3)
+        for b in range(BLOCKS):
+            empty(1, b)
+            scatter(1, b)

@@ -19,6 +19,7 @@ COPY = mybir.ActivationFunctionType.Copy
 P = 128
 PASSES = K // 512
 BLOCKS = N // P
+PAD = 16
 LIST_COLS = C // 16
 
 
@@ -46,9 +47,20 @@ def tile_routed_moe_kernel(tc, xT, w_words, w_scales, gate, offs, out):
         for u in range(2):
             for g in range(PASSES):
                 raw[g, u] = keep.tile([P, 2, T], F32, name="raw%d%d" % (g, u))
-                nc.sync.dma_start(raw[g, u][:], x_rows[g, :, 2 * u : 2 * u + 2, :])
-                if (g, u) == (0, 0):
-                    nc.sync.dma_start(offsets[:], offs)
+
+        def load_plane(g, t):
+            nc.sync.dma_start(raw[g, t // 2][:, t % 2, :], x_rows[g, :, t, :])
+
+        def load_pair(g, u):
+            nc.sync.dma_start(raw[g, u][:], x_rows[g, :, 2 * u : 2 * u + 2, :])
+
+        load_plane(0, 0)
+        load_plane(0, 1)
+        nc.sync.dma_start(offsets[:], offs)
+        load_pair(1, 0)
+        load_plane(0, 2)
+        load_plane(0, 3)
+        load_pair(1, 1)
 
         s_rows = w_scales.rearrange("e a q n -> (e a) q n")
         for q in range(4):
@@ -58,15 +70,24 @@ def tile_routed_moe_kernel(tc, xT, w_words, w_scales, gate, offs, out):
             )
         w_codes = keep.tile([P, E * PASSES, N], U32, name="w_codes", align_bytes=64)
         gates = keep.tile([P, BLOCKS, E * C], F32, name="gates")
-        nc.sync.dma_start(
-            w_codes[:, 0:PASSES, :].bitcast(I32),
-            w_words[0].rearrange("a p n r -> p a (n r)").bitcast(I32),
-        )
-        nc.sync.dma_start(gates[:], gate.rearrange("(b p) j -> p b j", p=P))
-        nc.sync.dma_start(
-            w_codes[:, PASSES : 2 * PASSES, :].bitcast(I32),
-            w_words[1].rearrange("a p n r -> p a (n r)").bitcast(I32),
-        )
+
+        def load_codes(e, a):
+            nc.sync.dma_start(
+                w_codes[:, e * PASSES + a, :].bitcast(I32),
+                w_words[e, a].rearrange("p n r -> p (n r)").bitcast(I32),
+            )
+
+        def load_gate(b):
+            nc.sync.dma_start(gates[:, b, :], gate[b * P : (b + 1) * P, :])
+
+        load_codes(0, 1)
+        load_codes(0, 0)
+        load_gate(0)
+        load_gate(1)
+        load_codes(1, 1)
+        load_codes(1, 0)
+        load_gate(2)
+        load_gate(3)
 
         grouped = {}
         x_codes = {}
@@ -75,39 +96,37 @@ def tile_routed_moe_kernel(tc, xT, w_words, w_scales, gate, offs, out):
         def new_grouped(g, e, tag):
             grouped[g, e] = keep.tile([P, C, 4], BF16, name="grouped%d%d" % (g, e), tag=tag, align_bytes=64)
 
+        for g in range(PASSES):
+            for e in range(E):
+                new_grouped(g, e, "grouped%d%d" % (g, e))
+
         planes = {}
-
-        def plane_cast(u):
-            planes[u] = keep.tile([P, 2, T], BF16, name="planes%d" % u, tag="planes%d" % u, align_bytes=64)
-            if u == 0:
-                nc.vector.tensor_copy(out=planes[u][:], in_=raw[0, u][:])
-            else:
-                nc.gpsimd.tensor_scalar(planes[u][:], raw[0, u][:], 1.0, 0.0, MULT, ADD)
-
-        def scalar_gather(e, u):
-            for h in range(2):
-                nc.scalar.activation(grouped[0, e][:, :, 2 * u + h], planes[u][:, h, :].indirect(slots(e)), COPY)
-
+        for u in range(2):
+            planes[u] = keep.tile([P, 2 * T + PAD], BF16, name="planes%d" % u, align_bytes=64)
         pair = {}
+        for u in range(2):
+            pair[u] = keep.tile([P, T + PAD // 2, 2], BF16, name="pair%d" % u, align_bytes=64)
+
+        def plane_cast(t, engine):
+            u, h = t // 2, t % 2
+            dst = planes[u][:, h * T : (h + 1) * T]
+            if engine == "vector":
+                nc.vector.tensor_copy(out=dst, in_=raw[0, u][:, h, :])
+            else:
+                nc.gpsimd.tensor_scalar(dst, raw[0, u][:, h, :], 1.0, 0.0, MULT, ADD)
+
+        def scalar_gather(e, t, pad=0):
+            u, h = t // 2, t % 2
+            window = planes[u][:, h * T : (h + 1) * T + pad]
+            nc.scalar.activation(grouped[0, e][:, :, t], window.indirect(slots(e)), COPY)
 
         def pair_cast(u):
-            pair[u] = keep.tile([P, T, 2], BF16, name="pair%d" % u, align_bytes=64)
-            nc.vector.tensor_copy(out=pair[u][:], in_=raw[1, u][:].rearrange("p h n -> p n h"))
+            nc.vector.tensor_copy(out=pair[u][:, 0:T, :], in_=raw[1, u][:].rearrange("p h n -> p n h"))
 
-        def vector_gather(e, u):
+        def vector_gather(e, u, pad=0):
             words = grouped[1, e][:].rearrange("p c t -> p (c t)").bitcast(U32)
-            nc.vector.tensor_copy(
-                words.rearrange("p (c u) -> p c u", u=2)[:, :, u],
-                pair[u][:].rearrange("p n h -> p (n h)").bitcast(U32).indirect(slots(e)),
-            )
-
-        def late_planes():
-            planes[2] = keep.tile([P, 2, T], BF16, name="planes2", align_bytes=64)
-            nc.gpsimd.tensor_scalar(planes[2][:], raw[1, 1][:], 1.0, 0.0, MULT, ADD)
-
-        def late_gather():
-            for h in range(2):
-                nc.scalar.activation(grouped[1, 1][:, :, 2 + h], planes[2][:, h, :].indirect(slots(1)), COPY)
+            window = pair[u][:].rearrange("p n h -> p (n h)").bitcast(U32)[:, 0 : T + pad // 2]
+            nc.vector.tensor_copy(words.rearrange("p (c u) -> p c u", u=2)[:, :, u], window.indirect(slots(e)))
 
         def quantize(g, e, tag):
             x_codes[g, e] = keep.tile([P, C], U32, name="x_codes%d%d" % (g, e), tag=tag, align_bytes=64)
@@ -136,17 +155,13 @@ def tile_routed_moe_kernel(tc, xT, w_words, w_scales, gate, offs, out):
                 stop=not opens,
             )
 
-        def multiply(e, g, opens):
-            for b in range(BLOCKS):
-                multiply_block(e, g, b, opens)
-
         windows = {}
         for b in range(BLOCKS):
             windows[b] = keep.tile([P, T], F32, name="window%d" % b)
         sums = {}
 
         def empty(e, b):
-            sums[e, b] = keep.tile([P, C], F32, name="sums%d%d" % (e, b), tag=("planes1" if (e, b) == (0, 3) else "sums%d%d" % (e, b)), align_bytes=64)
+            sums[e, b] = keep.tile([P, C], F32, name="sums%d%d" % (e, b), align_bytes=64)
             nc.scalar.copy(sums[e, b][:], acc[e, b][:])
 
         def scatter(e, b):
@@ -154,40 +169,47 @@ def tile_routed_moe_kernel(tc, xT, w_words, w_scales, gate, offs, out):
             if e == E - 1:
                 nc.sync.dma_start(out[b * P : (b + 1) * P, :], windows[b][:])
 
-        new_grouped(0, 0, "slot_b")
-        new_grouped(1, 0, "slot_a")
-        plane_cast(0)
+        plane_cast(0, "vector")
         scalar_gather(0, 0)
+        plane_cast(1, "vector")
+        scalar_gather(0, 1)
         pair_cast(0)
         vector_gather(0, 0)
-        new_grouped(1, 1, "slot_d")
+        scalar_gather(1, 0)
         vector_gather(1, 0)
-        plane_cast(1)
-        scalar_gather(0, 1)
+        plane_cast(2, "gpsimd")
+        plane_cast(3, "gpsimd")
+        scalar_gather(0, 2)
+        scalar_gather(0, 3)
+        nc.gpsimd.tensor_copy(planes[0][:, 2 * T : 2 * T + 1], grouped[0, 0][:, 0:1, 3])
+        nc.gpsimd.tensor_copy(pair[1][:, T : T + 1, 0], grouped[0, 0][:, 0:1, 3])
         pair_cast(1)
-        late_planes()
         vector_gather(0, 1)
-        quantize(1, 0, "slot_c")
+        quantize(1, 0, "x_codes10")
         multiply_block(0, 1, 0, True)
-        quantize(0, 0, "slot_a")
+        quantize(0, 0, "grouped10")
         multiply_block(0, 0, 0, False)
         for b in range(1, BLOCKS):
             multiply_block(0, 0, b, True)
             multiply_block(0, 1, b, False)
-        late_gather()
-        quantize(1, 1, "codes11")
-        multiply(1, 1, True)
-        for b in range(BLOCKS - 1):
-            empty(0, b)
-        new_grouped(0, 1, "slot_c")
-        scalar_gather(1, 0)
-        scalar_gather(1, 1)
-        empty(0, 3)
+        scalar_gather(1, 1, PAD)
+        scalar_gather(1, 2)
+        vector_gather(1, 1, PAD)
+        quantize(1, 1, "x_codes11")
+        empty(0, 0)
+        empty(0, 1)
+        nc.gpsimd.tensor_copy(planes[1][:, 2 * T : 2 * T + 1], sums[0, 1][:, 0:1])
         scatter(0, 0)
+        for b in range(BLOCKS):
+            multiply_block(1, 1, b, True)
+        scalar_gather(1, 3, PAD)
+        empty(0, 2)
         scatter(0, 1)
+        quantize(0, 1, "x_codes01")
+        for b in range(BLOCKS):
+            multiply_block(1, 0, b, False)
+        empty(0, 3)
         scatter(0, 2)
-        quantize(0, 1, "codes01")
-        multiply(1, 0, False)
         scatter(0, 3)
         for b in range(BLOCKS):
             empty(1, b)

@@ -48,18 +48,13 @@ def tile_routed_moe_kernel(tc, xT, w_words, w_scales, gate, offs, out):
             for g in range(PASSES):
                 raw[g, u] = keep.tile([P, 2, T], F32, name="raw%d%d" % (g, u))
 
-        def load_plane(g, t):
-            nc.sync.dma_start(raw[g, t // 2][:, t % 2, :], x_rows[g, :, t, :])
-
         def load_pair(g, u):
             nc.sync.dma_start(raw[g, u][:], x_rows[g, :, 2 * u : 2 * u + 2, :])
 
-        load_plane(0, 0)
-        load_plane(0, 1)
+        load_pair(0, 0)
         nc.sync.dma_start(offsets[:], offs)
         load_pair(1, 0)
-        load_plane(0, 2)
-        load_plane(0, 3)
+        load_pair(0, 1)
         load_pair(1, 1)
 
         s_rows = w_scales.rearrange("e a q n -> (e a) q n")
@@ -71,23 +66,15 @@ def tile_routed_moe_kernel(tc, xT, w_words, w_scales, gate, offs, out):
         w_codes = keep.tile([P, E * PASSES, N], U32, name="w_codes", align_bytes=64)
         gates = keep.tile([P, BLOCKS, E * C], F32, name="gates")
 
-        def load_codes(e, a):
-            nc.sync.dma_start(
-                w_codes[:, e * PASSES + a, :].bitcast(I32),
-                w_words[e, a].rearrange("p n r -> p (n r)").bitcast(I32),
-            )
-
-        def load_gate(b):
-            nc.sync.dma_start(gates[:, b, :], gate[b * P : (b + 1) * P, :])
-
-        load_codes(0, 1)
-        load_codes(0, 0)
-        load_gate(0)
-        load_gate(1)
-        load_codes(1, 1)
-        load_codes(1, 0)
-        load_gate(2)
-        load_gate(3)
+        nc.sync.dma_start(
+            w_codes[:, 0:PASSES, :].bitcast(I32),
+            w_words[0].rearrange("a p n r -> p a (n r)").bitcast(I32),
+        )
+        nc.sync.dma_start(gates[:], gate.rearrange("(b p) j -> p b j", p=P))
+        nc.sync.dma_start(
+            w_codes[:, PASSES : 2 * PASSES, :].bitcast(I32),
+            w_words[1].rearrange("a p n r -> p a (n r)").bitcast(I32),
+        )
 
         grouped = {}
         x_codes = {}

@@ -148,7 +148,7 @@ def tile_routed_moe_kernel(tc, xT, w_words, w_scales, gate, offs, out):
         sums = {}
 
         def empty(e, b):
-            sums[e, b] = keep.tile([P, C], F32, name="sums%d%d" % (e, b), align_bytes=64)
+            sums[e, b] = keep.tile([P, C], F32, name="sums%d%d" % (e, b), tag="sums%d%d" % (e, b), align_bytes=64)
             nc.scalar.copy(sums[e, b][:], acc[e, b][:])
 
         def scatter(e, b):
@@ -192,7 +192,7 @@ def tile_routed_moe_kernel(tc, xT, w_words, w_scales, gate, offs, out):
         scalar_gather(1, 3, PAD)
         empty(0, 2)
         scatter(0, 1)
-        quantize(0, 1, "x_codes01")
+        quantize(0, 1, "sums00")
         for b in range(BLOCKS):
             multiply_block(1, 0, b, False)
         empty(0, 3)

@@ -20,6 +20,7 @@ P = 128
 PASSES = K // 512
 BLOCKS = N // P
 PAD = 16
+PLANE_AT = (0, T, 2 * T + PAD, 3 * T + 2 * PAD)
 LIST_COLS = C // 16
 
 
@@ -87,24 +88,21 @@ def tile_routed_moe_kernel(tc, xT, w_words, w_scales, gate, offs, out):
             for e in range(E):
                 new_grouped(g, e, "grouped%d%d" % (g, e))
 
-        planes = {}
-        for u in range(2):
-            planes[u] = keep.tile([P, 2 * T + PAD], BF16, name="planes%d" % u, align_bytes=64)
+        planes = keep.tile([P, 4 * T + 3 * PAD], BF16, name="planes", align_bytes=64)
         pair = {}
         for u in range(2):
             pair[u] = keep.tile([P, T + PAD // 2, 2], BF16, name="pair%d" % u, align_bytes=64)
 
         def plane_cast(t, engine):
             u, h = t // 2, t % 2
-            dst = planes[u][:, h * T : (h + 1) * T]
+            dst = planes[:, PLANE_AT[t] : PLANE_AT[t] + T]
             if engine == "vector":
                 nc.vector.tensor_copy(out=dst, in_=raw[0, u][:, h, :])
             else:
                 nc.gpsimd.tensor_scalar(dst, raw[0, u][:, h, :], 1.0, 0.0, MULT, ADD)
 
-        def scalar_gather(e, t, pad=0):
-            u, h = t // 2, t % 2
-            window = planes[u][:, h * T : (h + 1) * T + pad]
+        def scalar_gather(e, t, stop):
+            window = planes[:, PLANE_AT[t] : stop]
             nc.scalar.activation(grouped[0, e][:, :, t], window.indirect(slots(e)), COPY)
 
         def pair_cast(u):
@@ -157,18 +155,14 @@ def tile_routed_moe_kernel(tc, xT, w_words, w_scales, gate, offs, out):
                 nc.sync.dma_start(out[b * P : (b + 1) * P, :], windows[b][:])
 
         plane_cast(0, "vector")
-        scalar_gather(0, 0)
         plane_cast(1, "vector")
-        scalar_gather(0, 1)
         pair_cast(0)
         vector_gather(0, 0)
-        scalar_gather(1, 0)
         vector_gather(1, 0)
         plane_cast(2, "gpsimd")
         plane_cast(3, "gpsimd")
-        scalar_gather(0, 2)
-        scalar_gather(0, 3)
-        nc.gpsimd.tensor_copy(planes[0][:, 2 * T : 2 * T + 1], grouped[0, 0][:, 0:1, 3])
+        for t in range(4):
+            scalar_gather(0, t, PLANE_AT[t] + T)
         nc.gpsimd.tensor_copy(pair[1][:, T : T + 1, 0], grouped[0, 0][:, 0:1, 3])
         pair_cast(1)
         vector_gather(0, 1)
@@ -179,23 +173,25 @@ def tile_routed_moe_kernel(tc, xT, w_words, w_scales, gate, offs, out):
         for b in range(1, BLOCKS):
             multiply_block(0, 0, b, True)
             multiply_block(0, 1, b, False)
-        scalar_gather(1, 1, PAD)
-        scalar_gather(1, 2)
+        scalar_gather(1, 0, PLANE_AT[3] + PAD)
         vector_gather(1, 1, PAD)
         quantize(1, 1, "x_codes11")
         empty(0, 0)
         empty(0, 1)
-        nc.gpsimd.tensor_copy(planes[1][:, 2 * T : 2 * T + 1], sums[0, 1][:, 0:1])
+        pads = planes[:, T:].rearrange("p (h n) -> p h n", h=3)[:, :, T : T + 2]
+        nc.gpsimd.tensor_copy(pads, sums[0, 0][:, 0:6].rearrange("p (h n) -> p h n", h=3))
         scatter(0, 0)
         for b in range(BLOCKS):
             multiply_block(1, 1, b, True)
-        scalar_gather(1, 3, PAD)
+        scalar_gather(1, 1, PLANE_AT[1] + T + PAD)
+        scalar_gather(1, 2, PLANE_AT[2] + T + PAD)
         empty(0, 2)
+        scalar_gather(1, 3, PLANE_AT[3] + T + PAD)
+        empty(0, 3)
         scatter(0, 1)
         quantize(0, 1, "sums00")
         for b in range(BLOCKS):
             multiply_block(1, 0, b, False)
-        empty(0, 3)
         scatter(0, 2)
         scatter(0, 3)
         for b in range(BLOCKS):

@@ -163,7 +163,7 @@ def tile_routed_moe_kernel(tc, xT, w_words, w_scales, gate, offs, out):
         plane_cast(3, "gpsimd")
         for t in range(4):
             scalar_gather(0, t, PLANE_AT[t] + T)
-        nc.gpsimd.tensor_copy(pair[1][:, T : T + 1, 0], grouped[0, 0][:, 0:1, 3])
+        nc.scalar.copy(pair[1][:, T : T + 1, 0], grouped[0, 0][:, 0:1, 3])
         pair_cast(1)
         vector_gather(0, 1)
         quantize(1, 0, "x_codes10")
@@ -179,7 +179,7 @@ def tile_routed_moe_kernel(tc, xT, w_words, w_scales, gate, offs, out):
         empty(0, 0)
         empty(0, 1)
         pads = planes[:, T:].rearrange("p (h n) -> p h n", h=3)[:, :, T : T + 2]
-        nc.gpsimd.tensor_copy(pads, sums[0, 0][:, 0:6].rearrange("p (h n) -> p h n", h=3))
+        nc.scalar.copy(pads, sums[0, 0][:, 0:6].rearrange("p (h n) -> p h n", h=3))
         scatter(0, 0)
         for b in range(BLOCKS):
             multiply_block(1, 1, b, True)

@@ -81,17 +81,21 @@ def tile_routed_moe_kernel(tc, xT, w_words, w_scales, gate, offs, out):
         x_codes = {}
         x_planes = {}
 
-        def new_grouped(g, e, tag):
-            grouped[g, e] = keep.tile([P, C, 4], BF16, name="grouped%d%d" % (g, e), tag=tag, align_bytes=64)
+        def new_grouped(g, e):
+            tile = keep.tile([P, C * 4], BF16, name="grouped%d%d" % (g, e), tag="grouped%d%d" % (g, e), align_bytes=64)
+            grouped[g, e] = tile[:]
 
-        for g in range(PASSES):
-            for e in range(E):
-                new_grouped(g, e, "grouped%d%d" % (g, e))
+        new_grouped(1, 0)
+        new_grouped(0, 1)
+        new_grouped(1, 1)
 
         planes = keep.tile([P, 4 * T + 3 * PAD], BF16, name="planes", align_bytes=64)
         pair = {}
-        for u in range(2):
-            pair[u] = keep.tile([P, T + PAD // 2, 2], BF16, name="pair%d" % u, align_bytes=64)
+        first_pair = keep.tile([P, 2 * T], BF16, name="first_pair", align_bytes=64)
+        second_pair = keep.tile([P, 2 * T + 4 * C], BF16, name="second_pair", align_bytes=64)
+        pair[0] = first_pair[:]
+        pair[1] = second_pair[:]
+        grouped[0, 0] = second_pair[:, 2 * T :]
 
         def plane_cast(t, engine):
             u, h = t // 2, t % 2
@@ -103,14 +107,14 @@ def tile_routed_moe_kernel(tc, xT, w_words, w_scales, gate, offs, out):
 
         def scalar_gather(e, t, stop):
             window = planes[:, PLANE_AT[t] : stop]
-            nc.scalar.activation(grouped[0, e][:, :, t], window.indirect(slots(e)), COPY)
+            nc.scalar.activation(grouped[0, e].rearrange("p (c t) -> p c t", t=4)[:, :, t], window.indirect(slots(e)), COPY)
 
         def pair_cast(u):
-            nc.vector.tensor_copy(out=pair[u][:, 0:T, :], in_=raw[1, u][:].rearrange("p h n -> p n h"))
+            nc.vector.tensor_copy(out=pair[u][:, 0 : 2 * T].rearrange("p (n h) -> p n h", h=2), in_=raw[1, u][:].rearrange("p h n -> p n h"))
 
         def vector_gather(e, u, pad=0):
-            words = grouped[1, e][:].rearrange("p c t -> p (c t)").bitcast(U32)
-            window = pair[u][:].rearrange("p n h -> p (n h)").bitcast(U32)[:, 0 : T + pad // 2]
+            words = grouped[1, e].bitcast(U32)
+            window = pair[u][:, 0 : 2 * T + pad].bitcast(U32)
             nc.vector.tensor_copy(words.rearrange("p (c u) -> p c u", u=2)[:, :, u], window.indirect(slots(e)))
 
         def quantize(g, e, tag):
@@ -119,7 +123,7 @@ def tile_routed_moe_kernel(tc, xT, w_words, w_scales, gate, offs, out):
             nc.vector.quantize_mx(
                 out=x_codes[g, e][:].bitcast(FP8X4),
                 scales=x_planes[g, e][:],
-                in_=grouped[g, e][:].rearrange("p c t -> p (c t)"),
+                in_=grouped[g, e],
             )
 
         acc = {}
@@ -163,7 +167,6 @@ def tile_routed_moe_kernel(tc, xT, w_words, w_scales, gate, offs, out):
         plane_cast(3, "gpsimd")
         for t in range(4):
             scalar_gather(0, t, PLANE_AT[t] + T)
-        nc.scalar.copy(pair[1][:, T : T + 1, 0], grouped[0, 0][:, 0:1, 3])
         pair_cast(1)
         vector_gather(0, 1)
         quantize(1, 0, "x_codes10")
@@ -189,7 +192,7 @@ def tile_routed_moe_kernel(tc, xT, w_words, w_scales, gate, offs, out):
         scalar_gather(1, 3, PLANE_AT[3] + T + PAD)
         empty(0, 3)
         scatter(0, 1)
-        quantize(0, 1, "sums00")
+        quantize(0, 1, "sums01")
         for b in range(BLOCKS):
             multiply_block(1, 0, b, False)
         scatter(0, 2)

@@ -20,7 +20,8 @@ P = 128
 PASSES = K // 512
 BLOCKS = N // P
 PAD = 16
-PLANE_AT = (0, T, 2 * T + PAD, 3 * T + 2 * PAD)
+PLANE_AT = (3 * T + PAD, 2 * T, 4 * T + PAD, 5 * T + PAD)
+PAD_STEP = 3 * T + PAD
 LIST_COLS = C // 16
 
 
@@ -52,9 +53,9 @@ def tile_routed_moe_kernel(tc, xT, w_words, w_scales, gate, offs, out):
         def load_pair(g, u):
             nc.sync.dma_start(raw[g, u][:], x_rows[g, :, 2 * u : 2 * u + 2, :])
 
-        load_pair(0, 0)
-        nc.sync.dma_start(offsets[:], offs)
         load_pair(1, 0)
+        nc.sync.dma_start(offsets[:], offs)
+        load_pair(0, 0)
         load_pair(0, 1)
         load_pair(1, 1)
 
@@ -89,11 +90,10 @@ def tile_routed_moe_kernel(tc, xT, w_words, w_scales, gate, offs, out):
         new_grouped(0, 1)
         new_grouped(1, 1)
 
-        planes = keep.tile([P, 4 * T + 3 * PAD], BF16, name="planes", align_bytes=64)
+        planes = keep.tile([P, 2 * PAD_STEP], BF16, name="planes", align_bytes=64)
         pair = {}
-        first_pair = keep.tile([P, 2 * T], BF16, name="first_pair", align_bytes=64)
         second_pair = keep.tile([P, 2 * T + 4 * C], BF16, name="second_pair", align_bytes=64)
-        pair[0] = first_pair[:]
+        pair[0] = planes[:]
         pair[1] = second_pair[:]
         grouped[0, 0] = second_pair[:, 2 * T :]
 
@@ -158,11 +158,11 @@ def tile_routed_moe_kernel(tc, xT, w_words, w_scales, gate, offs, out):
             if e == E - 1:
                 nc.sync.dma_start(out[b * P : (b + 1) * P, :], windows[b][:])
 
-        plane_cast(0, "vector")
-        plane_cast(1, "vector")
         pair_cast(0)
         vector_gather(0, 0)
-        vector_gather(1, 0)
+        plane_cast(0, "vector")
+        plane_cast(1, "vector")
+        vector_gather(1, 0, PAD)
         plane_cast(2, "gpsimd")
         plane_cast(3, "gpsimd")
         for t in range(4):
@@ -181,13 +181,13 @@ def tile_routed_moe_kernel(tc, xT, w_words, w_scales, gate, offs, out):
         quantize(1, 1, "x_codes11")
         empty(0, 0)
         empty(0, 1)
-        pads = planes[:, T:].rearrange("p (h n) -> p h n", h=3)[:, :, T : T + 2]
-        nc.scalar.copy(pads, sums[0, 0][:, 0:6].rearrange("p (h n) -> p h n", h=3))
+        pads = planes[:].rearrange("p (h n) -> p h n", h=2)[:, :, 3 * T : 3 * T + 2]
+        nc.scalar.copy(pads, sums[0, 0][:, 0:4].rearrange("p (h n) -> p h n", h=2))
         scatter(0, 0)
         for b in range(BLOCKS):
             multiply_block(1, 1, b, True)
         scalar_gather(1, 1, PLANE_AT[1] + T + PAD)
-        scalar_gather(1, 2, PLANE_AT[2] + T + PAD)
+        scalar_gather(1, 2, PLANE_AT[3] + T + PAD)
         empty(0, 2)
         scalar_gather(1, 3, PLANE_AT[3] + T + PAD)
         empty(0, 3)

from contextlib import ExitStack

import concourse.mybir as mybir

K, T, E, C, N = 1024, 512, 2, 256, 512
FLOPS = 2 * K * N * E * C

F32 = mybir.dt.float32
BF16 = mybir.dt.bfloat16
U32 = mybir.dt.uint32
I32 = mybir.dt.int32
U16 = mybir.dt.uint16
U8 = mybir.dt.uint8
FP8X4 = mybir.dt.float8_e4m3fn_x4
MULT = mybir.AluOpType.mult
ADD = mybir.AluOpType.add
COPY = mybir.ActivationFunctionType.Copy

P = 128
PASSES = K // 512
BLOCKS = N // P
PAD = 16
PLANE_AT = (3 * T + PAD, 2 * T, 4 * T + PAD, 5 * T + PAD)
PAD_STEP = 3 * T + PAD
LIST_COLS = C // 16


def tile_routed_moe_kernel(tc, xT, w_words, w_scales, gate, offs, out):
    nc = tc.nc
    with ExitStack() as ctx:
        lists = ctx.enter_context(tc.tile_pool(name="lists", bufs=1))
        keep = ctx.enter_context(tc.tile_pool(name="keep", bufs=1))
        psum = ctx.enter_context(tc.psum_pool(name="psum", bufs=1))

        offsets = lists.tile([P, E * C // 16], U16, name="offsets")

        def slots(e):
            return offsets[:, e * LIST_COLS : (e + 1) * LIST_COLS]

        warm = keep.tile([P, 2], F32, name="warm")
        nc.vector.memset(warm[:, 0:1], 0.0)
        nc.scalar.copy(warm[:, 1:2], warm[:, 0:1])

        w_planes = keep.tile([P, N], U8, name="w_planes", align_bytes=64)
        nc.vector.memset(w_planes[:].bitcast(I32), 0)

        x_rows = xT.rearrange("(g p t) n -> g p t n", p=P, t=4)
        raw = {}
        for u in range(2):
            for g in range(PASSES):
                raw[g, u] = keep.tile([P, 2, T], F32, name="raw%d%d" % (g, u))

        def load_pair(g, u):
            nc.sync.dma_start(raw[g, u][:], x_rows[g, :, 2 * u : 2 * u + 2, :])

        load_pair(1, 0)
        nc.sync.dma_start(offsets[:], offs)
        load_pair(0, 0)
        load_pair(0, 1)
        load_pair(1, 1)

        s_rows = w_scales.rearrange("e a q n -> (e a) q n")
        for q in range(4):
            nc.sync.dma_start(
                w_planes[32 * q : 32 * q + 16, :].bitcast(I32),
                s_rows[:, 4 * q : 4 * q + 4, :].bitcast(I32),
            )
        w_codes = keep.tile([P, E * PASSES, N], U32, name="w_codes", align_bytes=64)
        gates = keep.tile([P, BLOCKS, E * C], F32, name="gates")

        nc.sync.dma_start(
            w_codes[:, 0:PASSES, :].bitcast(I32),
            w_words[0].rearrange("a p n r -> p a (n r)").bitcast(I32),
        )
        nc.sync.dma_start(gates[:], gate.rearrange("(b p) j -> p b j", p=P))
        nc.sync.dma_start(
            w_codes[:, PASSES : 2 * PASSES, :].bitcast(I32),
            w_words[1].rearrange("a p n r -> p a (n r)").bitcast(I32),
        )

        grouped = {}
        x_codes = {}
        x_planes = {}

        def new_grouped(g, e):
            tile = keep.tile([P, C * 4], BF16, name="grouped%d%d" % (g, e), tag="grouped%d%d" % (g, e), align_bytes=64)
            grouped[g, e] = tile[:]

        new_grouped(1, 0)
        new_grouped(0, 1)
        new_grouped(1, 1)

        planes = keep.tile([P, 2 * PAD_STEP], BF16, name="planes", align_bytes=64)
        pair = {}
        second_pair = keep.tile([P, 2 * T + 4 * C], BF16, name="second_pair", align_bytes=64)
        pair[0] = planes[:]
        pair[1] = second_pair[:]
        grouped[0, 0] = second_pair[:, 2 * T :]

        def plane_cast(t, engine):
            u, h = t // 2, t % 2
            dst = planes[:, PLANE_AT[t] : PLANE_AT[t] + T]
            if engine == "vector":
                nc.vector.tensor_copy(out=dst, in_=raw[0, u][:, h, :])
            else:
                nc.gpsimd.tensor_scalar(dst, raw[0, u][:, h, :], 1.0, 0.0, MULT, ADD)

        def scalar_gather(e, t, stop):
            window = planes[:, PLANE_AT[t] : stop]
            nc.scalar.activation(grouped[0, e].rearrange("p (c t) -> p c t", t=4)[:, :, t], window.indirect(slots(e)), COPY)

        def pair_cast(u):
            nc.vector.tensor_copy(out=pair[u][:, 0 : 2 * T].rearrange("p (n h) -> p n h", h=2), in_=raw[1, u][:].rearrange("p h n -> p n h"))

        def vector_gather(e, u, pad=0):
            words = grouped[1, e].bitcast(U32)
            window = pair[u][:, 0 : 2 * T + pad].bitcast(U32)
            nc.vector.tensor_copy(words.rearrange("p (c u) -> p c u", u=2)[:, :, u], window.indirect(slots(e)))

        def quantize(g, e, tag):
            x_codes[g, e] = keep.tile([P, C], U32, name="x_codes%d%d" % (g, e), tag=tag, align_bytes=64)
            x_planes[g, e] = keep.tile([P, C], U8, name="x_planes%d%d" % (g, e), align_bytes=64)
            nc.vector.quantize_mx(
                out=x_codes[g, e][:].bitcast(FP8X4),
                scales=x_planes[g, e][:],
                in_=grouped[g, e],
            )

        acc = {}
        for e in range(E):
            for b in range(BLOCKS):
                acc[e, b] = psum.tile([P, C], F32, name="acc%d%d" % (e, b))

        def multiply_block(e, g, b, opens):
            j = e * PASSES + g
            cols = slice(b * P, (b + 1) * P)
            nc.tensor.matmul_mx(
                out=acc[e, b][:],
                lhsT=w_codes[:, j, cols].bitcast(FP8X4),
                lhsT_scale=w_planes[4 * j : P, cols],
                rhs=x_codes[g, e][:].bitcast(FP8X4),
                rhs_scale=x_planes[g, e][:],
                start=opens,
                stop=not opens,
            )

        windows = {}
        for b in range(BLOCKS):
            windows[b] = keep.tile([P, T], F32, name="window%d" % b)
        sums = {}

        def empty(e, b):
            sums[e, b] = keep.tile([P, C], F32, name="sums%d%d" % (e, b), tag="sums%d%d" % (e, b), align_bytes=64)
            nc.scalar.copy(sums[e, b][:], acc[e, b][:])

        def scatter(e, b):
            nc.vector.tensor_tensor(windows[b][:].indirect(slots(e)), sums[e, b][:], gates[:, b, e * C : (e + 1) * C], MULT)
            if e == E - 1:
                nc.sync.dma_start(out[b * P : (b + 1) * P, :], windows[b][:])

        pair_cast(0)
        vector_gather(0, 0)
        plane_cast(0, "vector")
        plane_cast(1, "vector")
        vector_gather(1, 0, PAD)
        plane_cast(2, "gpsimd")
        plane_cast(3, "gpsimd")
        for t in range(4):
            scalar_gather(0, t, PLANE_AT[t] + T)
        pair_cast(1)
        vector_gather(0, 1)
        quantize(1, 0, "x_codes10")
        multiply_block(0, 1, 0, True)
        quantize(0, 0, "grouped10")
        multiply_block(0, 0, 0, False)
        for b in range(1, BLOCKS):
            multiply_block(0, 0, b, True)
            multiply_block(0, 1, b, False)
        scalar_gather(1, 0, PLANE_AT[3] + PAD)
        vector_gather(1, 1, PAD)
        quantize(1, 1, "x_codes11")
        empty(0, 0)
        empty(0, 1)
        pads = planes[:].rearrange("p (h n) -> p h n", h=2)[:, :, 3 * T : 3 * T + 2]
        nc.scalar.copy(pads, sums[0, 0][:, 0:4].rearrange("p (h n) -> p h n", h=2))
        scatter(0, 0)
        for b in range(BLOCKS):
            multiply_block(1, 1, b, True)
        scalar_gather(1, 1, PLANE_AT[1] + T + PAD)
        scalar_gather(1, 2, PLANE_AT[3] + T + PAD)
        empty(0, 2)
        scalar_gather(1, 3, PLANE_AT[3] + T + PAD)
        empty(0, 3)
        scatter(0, 1)
        quantize(0, 1, "sums01")
        for b in range(BLOCKS):
            multiply_block(1, 0, b, False)
        scatter(0, 2)
        scatter(0, 3)
        for b in range(BLOCKS):
            empty(1, b)
            scatter(1, b)
